import numpy as np
import ml_dtypes


def mxq(x, axis, fmt="e4m3"):
    dtype, down = {"e4m3": (ml_dtypes.float8_e4m3fn, 7), "e5m2": (ml_dtypes.float8_e5m2, 14)}[fmt]
    v = np.moveaxis(np.asarray(x, np.float32).astype(ml_dtypes.bfloat16).astype(np.float64), axis, -1)
    blocks = v.reshape(v.shape[:-1] + (-1, 32))
    amax = np.abs(blocks).max(-1, keepdims=True)
    byte = np.maximum(np.where(amax > 0, np.frexp(amax)[1] - 1 + 127, 0) - down, 1)
    scale = np.exp2(byte - 127.0)
    codes = (blocks / scale).astype(np.float32).astype(dtype).astype(np.float64)
    return np.moveaxis((codes * scale).reshape(v.shape), -1, axis)


WIDE = False


def mx_kscale(k):
    if not WIDE:
        return np.ones(k)
    levels = np.array([10, -10, 5, -5, 0])
    if k % 512:
        return np.exp2(np.random.permutation(np.resize(levels, k // 32))).repeat(32)
    a = np.empty((k // 512, 16))
    for p in range(k // 512):
        a[p, :8] = np.random.permutation(np.resize(levels, 8))
        for g in range(8):
            far = levels[np.abs(levels - a[p, g]) >= 10]
            a[p, g + 8] = far[np.random.randint(len(far))]
    return np.exp2(a.ravel()).repeat(32)


def f64(x):
    return np.asarray(x).astype(np.float64)


def striped(idx):
    return np.tile(idx.reshape(-1, 16).T, (8, 1)).astype(np.uint16)


def unstriped(offs):
    return offs[:16].T.reshape(-1).astype(np.int64)


def pack_weight(w):
    k, n = w.shape
    w = f64(np.asarray(w, np.float32).astype(ml_dtypes.bfloat16)).reshape(k // 32, 32, n)
    amax = np.abs(w).max(1)
    byte = np.clip(np.where(amax > 0, np.frexp(amax)[1] - 1 + 127 - 7, 1), 1, 254)
    scaled = (w * np.exp2(127.0 - byte)[:, None, :]).reshape(k, n).astype(np.float32)
    words = np.ascontiguousarray(scaled.reshape(k // 512, 128, 4, n).transpose(0, 1, 3, 2)).astype(ml_dtypes.float8_e4m3fn).view(np.uint8)
    return words, np.ascontiguousarray(byte.astype(np.uint8).reshape(k // 512, 16, n))


def unpack_weight(words, scales):
    g, p, n, _ = words.shape
    vals = np.ascontiguousarray(words).view(ml_dtypes.float8_e4m3fn).astype(np.float64) * np.repeat(np.exp2(scales.astype(np.float64) - 127.0), 8, axis=1)[..., None]
    return vals.transpose(0, 1, 3, 2).reshape(g * 512, n)


K, T, S, D, N, R = 512, 1024, 512, 4, 256, 256


def setup_inputs():
    n = np.random.standard_normal
    s = mx_kscale(K)[:, None]
    packed_xT = pack_weight(n((K, T)) * s)
    return {
        "x_words": packed_xT[0],
        "x_scales": packed_xT[1],
        "w1": (n((K, N)) / np.sqrt(K) / s).astype(np.float32),
        "flow": (n((N, R))).astype(np.float32),
        "offs": striped(np.random.permutation(T)[:S]),
        "nbr": striped(np.random.permutation(np.concatenate([np.arange(R), np.random.randint(0, R, S - R)]))),
    }


def reference(x_words, x_scales, w1, flow, offs, nbr):
    xq = unpack_weight(x_words, x_scales)[:, unstriped(offs)]
    y = mxq(f64(w1), 0, "e4m3").T @ xq
    top = y.reshape(len(y), -1, D).max(axis=2)
    ex = np.exp(y - np.repeat(top, D, axis=1))
    total = ex.reshape(len(ex), -1, D).sum(axis=2)
    mask = ex / np.repeat(total, D, axis=1)
    mf = mask * f64(flow)[:, unstriped(nbr)]
    return 8.0 * (mf.reshape(len(mf), -1, D).sum(axis=2))

@@ -1,0 +1,121 @@
+from contextlib import ExitStack
+
+import concourse.mybir as mybir
+
+K, T, S, D, N, R = 512, 1024, 512, 4, 256, 256
+P = 128
+V = S // D
+TILES = N // P
+HALVES = 2
+HALF = S // HALVES
+FLOW_WINDOW = S + 16
+FLOPS = 2 * K * N * S
+
+F32 = mybir.dt.float32
+BF16 = mybir.dt.bfloat16
+I32 = mybir.dt.int32
+U32 = mybir.dt.uint32
+U16 = mybir.dt.uint16
+U8 = mybir.dt.uint8
+FP8X4 = mybir.dt.float8_e4m3fn_x4
+ALU = mybir.AluOpType
+ACT = mybir.ActivationFunctionType
+AX = mybir.AxisListType
+
+
+def tile_picked_yraft_up_p_kernel(tc, x_words, x_scales, w1, flow, offs, nbr, out):
+    nc = tc.nc
+    with ExitStack() as ctx:
+        pool = ctx.enter_context(tc.tile_pool(name="held", bufs=1))
+        psum = ctx.enter_context(tc.psum_pool(name="psum", bufs=1))
+
+        offs_sb = pool.tile([P, S // 16], U16, name="offs_sb")
+        nbr_sb = pool.tile([P, S // 16], U16, name="nbr_sb")
+        word_table = pool.tile([P, T], I32, name="word_table")
+        byte_table = pool.tile([P, T], U8, name="byte_table")
+        w_raw = [pool.tile([P, 4, P], F32, name=f"w_raw{t}") for t in range(TILES)]
+        flow_table = [pool.tile([P, FLOW_WINDOW], F32, name=f"flow_table{t}") for t in range(TILES)]
+
+        nc.vector.memset(byte_table[:].bitcast(I32), 0)
+        nc.sync.dma_start(offs_sb[:], offs)
+        nc.sync.dma_start(w_raw[0][:], w1[:, 0:P].rearrange("(p j) c -> p j c", j=4))
+        for q in range(4):
+            nc.sync.dma_start(byte_table[32 * q : 32 * q + 4, :].bitcast(I32), x_scales[0, 4 * q : 4 * q + 4, :].bitcast(I32))
+        nc.sync.dma_start(w_raw[1][:], w1[:, P : 2 * P].rearrange("(p j) c -> p j c", j=4))
+        nc.sync.dma_start(word_table[:], x_words[0].rearrange("p n t -> p (n t)").bitcast(I32))
+        nc.sync.dma_start(nbr_sb[:], nbr)
+        for t in range(TILES):
+            nc.gpsimd.memset(flow_table[t][:, R:], 0.0)
+            nc.sync.dma_start(flow_table[t][:, 0:R], flow[t * P : (t + 1) * P, :])
+
+        x_bytes = pool.tile([P, S], U8, name="x_bytes", align_bytes=64)
+        nc.vector.tensor_copy(x_bytes[:], byte_table[:].indirect(offs_sb[:]))
+
+        w_codes, w_bytes = [], []
+
+        def quantise(t):
+            grouped = pool.tile([P, P, 4], BF16, name=f"grouped{t}", align_bytes=64)
+            nc.scalar.activation(
+                grouped[:].rearrange("p (c i) j -> p c j i", i=4),
+                w_raw[t][:].rearrange("p j (c i) -> p c j i", i=4),
+                ACT.Copy,
+            )
+            codes = pool.tile([P, P], U32, name=f"w_codes{t}", align_bytes=64)
+            scale = pool.tile([P, P], U8, name=f"w_bytes{t}", align_bytes=64)
+            nc.vector.quantize_mx(codes[:].bitcast(FP8X4), scale[:], grouped[:].rearrange("p c j -> p (c j)"))
+            w_codes.append(codes)
+            w_bytes.append(scale)
+
+        quantise(0)
+        quantise(1)
+        x_codes = []
+        for h in range(HALVES):
+            codes = pool.tile([P, HALF], U32, name=f"x_codes{h}", align_bytes=64)
+            cols = slice(h * HALF // 16, (h + 1) * HALF // 16)
+            nc.vector.tensor_copy(codes[:], word_table[:].bitcast(U32).indirect(offs_sb[:, cols]))
+            x_codes.append(codes)
+
+        ex = pool.tile([P, TILES, S], F32, name="ex")
+        mf = pool.tile([P, TILES, S], F32, name="mf")
+        total = pool.tile([P, TILES * V], F32, name="total")
+        num = pool.tile([P, TILES * V], F32, name="num")
+        for t in range(TILES):
+            ys, tops = [], []
+            for h in range(HALVES):
+                y = psum.tile([P, HALF], F32, name=f"y{t}{h}")
+                nc.tensor.matmul_mx(
+                    y[:],
+                    lhsT=w_codes[t][:].bitcast(FP8X4),
+                    lhsT_scale=w_bytes[t][:],
+                    rhs=x_codes[h][:].bitcast(FP8X4),
+                    rhs_scale=x_bytes[:, h * HALF : (h + 1) * HALF],
+                    start=True,
+                    stop=True,
+                )
+                top = pool.tile([P, HALF // D], F32, name=f"top{t}{h}")
+                nc.vector.tensor_reduce(top[:], y[:].rearrange("p (v d) -> p v d", d=D), AX.X, ALU.max)
+                ys.append(y)
+                tops.append(top)
+            for h in range(HALVES):
+                z = pool.tile([P, HALF // D, D], F32, name=f"z{t}{h}")
+                nc.vector.tensor_tensor(
+                    z[:],
+                    ys[h][:].rearrange("p (v d) -> p v d", d=D),
+                    tops[h][:].unsqueeze(2).to_broadcast([P, HALF // D, D]),
+                    ALU.subtract,
+                )
+                nc.scalar.activation(ex[:, t, h * HALF : (h + 1) * HALF], z[:].rearrange("p v d -> p (v d)"), ACT.Exp)
+        for t in range(TILES):
+            nc.vector.tensor_reduce(total[:, t * V : (t + 1) * V], ex[:, t, :].rearrange("p (v d) -> p v d", d=D), AX.X, ALU.add)
+        root = pool.tile([P, TILES * V], F32, name="root")
+        inverse = pool.tile([P, TILES * V], F32, name="inverse")
+        nc.scalar.activation(root[:], total[:], ACT.Abs_reciprocal_sqrt)
+        nc.scalar.activation(inverse[:], root[:], ACT.Square)
+        for t in range(TILES):
+            nc.vector.tensor_tensor(mf[:, t, :], flow_table[t][:].indirect(nbr_sb[:]), ex[:, t, :], ALU.mult)
+        result = pool.tile([P, TILES * V], F32, name="result")
+        for t in range(TILES):
+            cols = slice(t * V, (t + 1) * V)
+            nc.vector.tensor_reduce(num[:, cols], mf[:, t, :].rearrange("p (v d) -> p v d", d=D), AX.X, ALU.add)
+            nc.vector.scalar_tensor_tensor(result[:, cols], num[:, cols], 8.0, inverse[:, cols], ALU.mult, ALU.mult)
+            nc.sync.dma_start(out[t * P : (t + 1) * P, :], result[:, cols])

@@ -1,6 +1,7 @@
 from contextlib import ExitStack
 
 import concourse.mybir as mybir
+from concourse.masks import make_identity
 
 K, T, S, D, N, R = 512, 1024, 512, 4, 256, 256
 P = 128
@@ -35,18 +36,20 @@ def tile_picked_yraft_up_p_kernel(tc, x_words, x_scales, w1, flow, offs, nbr, ou
         byte_table = pool.tile([P, T], U8, name="byte_table")
         w_raw = [pool.tile([P, 4, P], F32, name=f"w_raw{t}") for t in range(TILES)]
         flow_table = [pool.tile([P, FLOW_WINDOW], F32, name=f"flow_table{t}") for t in range(TILES)]
+        identity = pool.tile([P, P], F32, name="identity")
 
         nc.vector.memset(byte_table[:].bitcast(I32), 0)
         nc.sync.dma_start(offs_sb[:], offs)
         nc.sync.dma_start(w_raw[0][:], w1[:, 0:P].rearrange("(p j) c -> p j c", j=4))
         for q in range(4):
             nc.sync.dma_start(byte_table[32 * q : 32 * q + 4, :].bitcast(I32), x_scales[0, 4 * q : 4 * q + 4, :].bitcast(I32))
-        nc.sync.dma_start(w_raw[1][:], w1[:, P : 2 * P].rearrange("(p j) c -> p j c", j=4))
         nc.sync.dma_start(word_table[:], x_words[0].rearrange("p n t -> p (n t)").bitcast(I32))
+        nc.sync.dma_start(w_raw[1][:], w1[:, P : 2 * P].rearrange("(p j) c -> p j c", j=4))
         nc.sync.dma_start(nbr_sb[:], nbr)
         for t in range(TILES):
             nc.gpsimd.memset(flow_table[t][:, R:], 0.0)
             nc.sync.dma_start(flow_table[t][:, 0:R], flow[t * P : (t + 1) * P, :])
+        make_identity(nc, identity[:])
 
         x_bytes = pool.tile([P, S], U8, name="x_bytes", align_bytes=64)
         nc.vector.tensor_copy(x_bytes[:], byte_table[:].indirect(offs_sb[:]))
@@ -54,7 +57,7 @@ def tile_picked_yraft_up_p_kernel(tc, x_words, x_scales, w1, flow, offs, nbr, ou
         w_codes, w_bytes = [], []
 
         def quantise(t):
-            grouped = pool.tile([P, P, 4], BF16, name=f"grouped{t}", align_bytes=64)
+            grouped = pool.tile([P, P, 4], BF16, name=f"grouped{t}", tag=f"grouped{t}", align_bytes=64)
             nc.scalar.activation(
                 grouped[:].rearrange("p (c i) j -> p c j i", i=4),
                 w_raw[t][:].rearrange("p j (c i) -> p c j i", i=4),
@@ -67,20 +70,20 @@ def tile_picked_yraft_up_p_kernel(tc, x_words, x_scales, w1, flow, offs, nbr, ou
             w_bytes.append(scale)
 
         quantise(0)
-        quantise(1)
         x_codes = []
         for h in range(HALVES):
             codes = pool.tile([P, HALF], U32, name=f"x_codes{h}", align_bytes=64)
             cols = slice(h * HALF // 16, (h + 1) * HALF // 16)
             nc.vector.tensor_copy(codes[:], word_table[:].bitcast(U32).indirect(offs_sb[:, cols]))
             x_codes.append(codes)
+        quantise(1)
 
+        top = pool.tile([P, TILES, HALVES, HALF // D], F32, name="top", tag=f"grouped{TILES - 1}", align_bytes=64)
         ex = pool.tile([P, TILES, S], F32, name="ex")
         mf = pool.tile([P, TILES, S], F32, name="mf")
-        total = pool.tile([P, TILES * V], F32, name="total")
         num = pool.tile([P, TILES * V], F32, name="num")
         for t in range(TILES):
-            ys, tops = [], []
+            ys = []
             for h in range(HALVES):
                 y = psum.tile([P, HALF], F32, name=f"y{t}{h}")
                 nc.tensor.matmul_mx(
@@ -92,30 +95,47 @@ def tile_picked_yraft_up_p_kernel(tc, x_words, x_scales, w1, flow, offs, nbr, ou
                     start=True,
                     stop=True,
                 )
-                top = pool.tile([P, HALF // D], F32, name=f"top{t}{h}")
-                nc.vector.tensor_reduce(top[:], y[:].rearrange("p (v d) -> p v d", d=D), AX.X, ALU.max)
+                nc.vector.tensor_reduce(top[:, t, h, :], y[:].rearrange("p (v d) -> p v d", d=D), AX.X, ALU.max)
                 ys.append(y)
-                tops.append(top)
             for h in range(HALVES):
                 z = pool.tile([P, HALF // D, D], F32, name=f"z{t}{h}")
                 nc.vector.tensor_tensor(
                     z[:],
                     ys[h][:].rearrange("p (v d) -> p v d", d=D),
-                    tops[h][:].unsqueeze(2).to_broadcast([P, HALF // D, D]),
+                    top[:, t, h, :].unsqueeze(2).to_broadcast([P, HALF // D, D]),
                     ALU.subtract,
                 )
                 nc.scalar.activation(ex[:, t, h * HALF : (h + 1) * HALF], z[:].rearrange("p v d -> p (v d)"), ACT.Exp)
+
+        total_t = psum.tile([P, TILES * P], F32, name="total_t")
         for t in range(TILES):
-            nc.vector.tensor_reduce(total[:, t * V : (t + 1) * V], ex[:, t, :].rearrange("p (v d) -> p v d", d=D), AX.X, ALU.add)
-        root = pool.tile([P, TILES * V], F32, name="root")
-        inverse = pool.tile([P, TILES * V], F32, name="inverse")
-        nc.scalar.activation(root[:], total[:], ACT.Abs_reciprocal_sqrt)
-        nc.scalar.activation(inverse[:], root[:], ACT.Square)
+            for d in range(D):
+                nc.tensor.matmul(
+                    total_t[:, t * P : (t + 1) * P],
+                    lhsT=ex[:, t, d:S:D],
+                    rhs=identity[:],
+                    start=(d == 0),
+                    stop=(d == D - 1),
+                    is_transpose=True,
+                )
+        root_t = pool.tile([P, TILES * P], F32, name="root_t")
+        inverse_t = pool.tile([P, TILES * P], F32, name="inverse_t")
+        for t in range(TILES):
+            cols = slice(t * P, (t + 1) * P)
+            nc.scalar.activation(root_t[:, cols], total_t[:, cols], ACT.Abs_reciprocal_sqrt)
+        inverse = []
+        for t in range(TILES):
+            cols = slice(t * P, (t + 1) * P)
+            nc.scalar.activation(inverse_t[:, cols], root_t[:, cols], ACT.Square)
+            back = psum.tile([P, V], F32, name=f"inverse{t}")
+            nc.tensor.transpose(back[:], inverse_t[:, cols], identity[:])
+            inverse.append(back)
         for t in range(TILES):
             nc.vector.tensor_tensor(mf[:, t, :], flow_table[t][:].indirect(nbr_sb[:]), ex[:, t, :], ALU.mult)
         result = pool.tile([P, TILES * V], F32, name="result")
         for t in range(TILES):
+            nc.vector.tensor_reduce(num[:, t * V : (t + 1) * V], mf[:, t, :].rearrange("p (v d) -> p v d", d=D), AX.X, ALU.add)
+        for t in range(TILES):
             cols = slice(t * V, (t + 1) * V)
-            nc.vector.tensor_reduce(num[:, cols], mf[:, t, :].rearrange("p (v d) -> p v d", d=D), AX.X, ALU.add)
-            nc.vector.scalar_tensor_tensor(result[:, cols], num[:, cols], 8.0, inverse[:, cols], ALU.mult, ALU.mult)
+            nc.vector.scalar_tensor_tensor(result[:, cols], num[:, cols], 8.0, inverse[t][:], ALU.mult, ALU.mult)
             nc.sync.dma_start(out[t * P : (t + 1) * P, :], result[:, cols])

@@ -47,9 +47,10 @@ def tile_picked_yraft_up_p_kernel(tc, x_words, x_scales, w1, flow, offs, nbr, ou
         nc.sync.dma_start(w_raw[1][:], w1[:, P : 2 * P].rearrange("(p j) c -> p j c", j=4))
         nc.sync.dma_start(nbr_sb[:], nbr)
         for t in range(TILES):
-            nc.gpsimd.memset(flow_table[t][:, R:], 0.0)
+            nc.vector.memset(flow_table[t][:, R:], 0.0)
             nc.sync.dma_start(flow_table[t][:, 0:R], flow[t * P : (t + 1) * P, :])
-        make_identity(nc, identity[:])
+        nc.vector.memset(identity[:], 0.0)
+        make_identity(nc, identity[:], nomemset=True)
 
         x_bytes = pool.tile([P, S], U8, name="x_bytes", align_bytes=64)
         nc.vector.tensor_copy(x_bytes[:], byte_table[:].indirect(offs_sb[:]))
@@ -79,8 +80,8 @@ def tile_picked_yraft_up_p_kernel(tc, x_words, x_scales, w1, flow, offs, nbr, ou
         quantise(1)
 
         top = pool.tile([P, TILES, HALVES, HALF // D], F32, name="top", tag=f"grouped{TILES - 1}", align_bytes=64)
-        ex = pool.tile([P, TILES, S], F32, name="ex")
-        mf = pool.tile([P, TILES, S], F32, name="mf")
+        ex = [pool.tile([P, S], F32, name=f"ex{t}") for t in range(TILES)]
+        mf = [pool.tile([P, S], F32, name=f"mf{t}") for t in range(TILES)]
         num = pool.tile([P, TILES * V], F32, name="num")
         for t in range(TILES):
             ys = []
@@ -105,14 +106,14 @@ def tile_picked_yraft_up_p_kernel(tc, x_words, x_scales, w1, flow, offs, nbr, ou
                     top[:, t, h, :].unsqueeze(2).to_broadcast([P, HALF // D, D]),
                     ALU.subtract,
                 )
-                nc.scalar.activation(ex[:, t, h * HALF : (h + 1) * HALF], z[:].rearrange("p v d -> p (v d)"), ACT.Exp)
+                nc.scalar.activation(ex[t][:, h * HALF : (h + 1) * HALF], z[:].rearrange("p v d -> p (v d)"), ACT.Exp)
 
         total_t = psum.tile([P, TILES * P], F32, name="total_t")
         for t in range(TILES):
             for d in range(D):
                 nc.tensor.matmul(
                     total_t[:, t * P : (t + 1) * P],
-                    lhsT=ex[:, t, d:S:D],
+                    lhsT=ex[t][:, d:S:D],
                     rhs=identity[:],
                     start=(d == 0),
                     stop=(d == D - 1),
@@ -131,10 +132,10 @@ def tile_picked_yraft_up_p_kernel(tc, x_words, x_scales, w1, flow, offs, nbr, ou
             nc.tensor.transpose(back[:], inverse_t[:, cols], identity[:])
             inverse.append(back)
         for t in range(TILES):
-            nc.vector.tensor_tensor(mf[:, t, :], flow_table[t][:].indirect(nbr_sb[:]), ex[:, t, :], ALU.mult)
+            nc.vector.tensor_tensor(mf[t][:], flow_table[t][:].indirect(nbr_sb[:]), ex[t][:], ALU.mult)
         result = pool.tile([P, TILES * V], F32, name="result")
         for t in range(TILES):
-            nc.vector.tensor_reduce(num[:, t * V : (t + 1) * V], mf[:, t, :].rearrange("p (v d) -> p v d", d=D), AX.X, ALU.add)
+            nc.vector.tensor_reduce(num[:, t * V : (t + 1) * V], mf[t][:].rearrange("p (v d) -> p v d", d=D), AX.X, ALU.add)
         for t in range(TILES):
             cols = slice(t * V, (t + 1) * V)
             nc.vector.scalar_tensor_tensor(result[:, cols], num[:, cols], 8.0, inverse[t][:], ALU.mult, ALU.mult)

from contextlib import ExitStack

import concourse.mybir as mybir
from concourse.masks import make_identity

K, T, S, D, N, R = 512, 1024, 512, 4, 256, 256
P = 128
V = S // D
TILES = N // P
HALVES = 2
HALF = S // HALVES
FLOW_WINDOW = S + 16
FLOPS = 2 * K * N * S

F32 = mybir.dt.float32
BF16 = mybir.dt.bfloat16
I32 = mybir.dt.int32
U32 = mybir.dt.uint32
U16 = mybir.dt.uint16
U8 = mybir.dt.uint8
FP8X4 = mybir.dt.float8_e4m3fn_x4
ALU = mybir.AluOpType
ACT = mybir.ActivationFunctionType
AX = mybir.AxisListType


def tile_picked_yraft_up_p_kernel(tc, x_words, x_scales, w1, flow, offs, nbr, out):
    nc = tc.nc
    with ExitStack() as ctx:
        pool = ctx.enter_context(tc.tile_pool(name="held", bufs=1))
        psum = ctx.enter_context(tc.psum_pool(name="psum", bufs=1))

        offs_sb = pool.tile([P, S // 16], U16, name="offs_sb")
        nbr_sb = pool.tile([P, S // 16], U16, name="nbr_sb")
        word_table = pool.tile([P, T], I32, name="word_table")
        byte_table = pool.tile([P, T], U8, name="byte_table")
        w_raw = [pool.tile([P, 4, P], F32, name=f"w_raw{t}") for t in range(TILES)]
        flow_table = [pool.tile([P, FLOW_WINDOW], F32, name=f"flow_table{t}") for t in range(TILES)]
        identity = pool.tile([P, P], F32, name="identity")

        nc.vector.memset(byte_table[:].bitcast(I32), 0)
        nc.sync.dma_start(offs_sb[:], offs)
        nc.sync.dma_start(w_raw[0][:], w1[:, 0:P].rearrange("(p j) c -> p j c", j=4))
        for q in range(4):
            nc.sync.dma_start(byte_table[32 * q : 32 * q + 4, :].bitcast(I32), x_scales[0, 4 * q : 4 * q + 4, :].bitcast(I32))
        nc.sync.dma_start(word_table[:], x_words[0].rearrange("p n t -> p (n t)").bitcast(I32))
        nc.sync.dma_start(w_raw[1][:], w1[:, P : 2 * P].rearrange("(p j) c -> p j c", j=4))
        nc.sync.dma_start(nbr_sb[:], nbr)
        for t in range(TILES):
            nc.vector.memset(flow_table[t][:, R:], 0.0)
            nc.sync.dma_start(flow_table[t][:, 0:R], flow[t * P : (t + 1) * P, :])
        nc.vector.memset(identity[:], 0.0)
        make_identity(nc, identity[:], nomemset=True)

        x_bytes = pool.tile([P, S], U8, name="x_bytes", align_bytes=64)
        nc.vector.tensor_copy(x_bytes[:], byte_table[:].indirect(offs_sb[:]))

        w_codes, w_bytes = [], []

        def quantise(t):
            grouped = pool.tile([P, P, 4], BF16, name=f"grouped{t}", tag=f"grouped{t}", align_bytes=64)
            nc.scalar.activation(
                grouped[:].rearrange("p (c i) j -> p c j i", i=4),
                w_raw[t][:].rearrange("p j (c i) -> p c j i", i=4),
                ACT.Copy,
            )
            codes = pool.tile([P, P], U32, name=f"w_codes{t}", align_bytes=64)
            scale = pool.tile([P, P], U8, name=f"w_bytes{t}", align_bytes=64)
            nc.vector.quantize_mx(codes[:].bitcast(FP8X4), scale[:], grouped[:].rearrange("p c j -> p (c j)"))
            w_codes.append(codes)
            w_bytes.append(scale)

        quantise(0)
        x_codes = []
        for h in range(HALVES):
            codes = pool.tile([P, HALF], U32, name=f"x_codes{h}", align_bytes=64)
            cols = slice(h * HALF // 16, (h + 1) * HALF // 16)
            nc.vector.tensor_copy(codes[:], word_table[:].bitcast(U32).indirect(offs_sb[:, cols]))
            x_codes.append(codes)
        quantise(1)

        top = pool.tile([P, TILES, HALVES, HALF // D], F32, name="top", tag=f"grouped{TILES - 1}", align_bytes=64)
        ex = [pool.tile([P, S], F32, name=f"ex{t}") for t in range(TILES)]
        mf = [pool.tile([P, S], F32, name=f"mf{t}") for t in range(TILES)]
        num = pool.tile([P, TILES * V], F32, name="num")
        for t in range(TILES):
            ys = []
            for h in range(HALVES):
                y = psum.tile([P, HALF], F32, name=f"y{t}{h}")
                nc.tensor.matmul_mx(
                    y[:],
                    lhsT=w_codes[t][:].bitcast(FP8X4),
                    lhsT_scale=w_bytes[t][:],
                    rhs=x_codes[h][:].bitcast(FP8X4),
                    rhs_scale=x_bytes[:, h * HALF : (h + 1) * HALF],
                    start=True,
                    stop=True,
                )
                nc.vector.tensor_reduce(top[:, t, h, :], y[:].rearrange("p (v d) -> p v d", d=D), AX.X, ALU.max)
                ys.append(y)
            for h in range(HALVES):
                z = pool.tile([P, HALF // D, D], F32, name=f"z{t}{h}")
                nc.vector.tensor_tensor(
                    z[:],
                    ys[h][:].rearrange("p (v d) -> p v d", d=D),
                    top[:, t, h, :].unsqueeze(2).to_broadcast([P, HALF // D, D]),
                    ALU.subtract,
                )
                nc.scalar.activation(ex[t][:, h * HALF : (h + 1) * HALF], z[:].rearrange("p v d -> p (v d)"), ACT.Exp)

        total_t = psum.tile([P, TILES * P], F32, name="total_t")
        for t in range(TILES):
            for d in range(D):
                nc.tensor.matmul(
                    total_t[:, t * P : (t + 1) * P],
                    lhsT=ex[t][:, d:S:D],
                    rhs=identity[:],
                    start=(d == 0),
                    stop=(d == D - 1),
                    is_transpose=True,
                )
        root_t = pool.tile([P, TILES * P], F32, name="root_t")
        inverse_t = pool.tile([P, TILES * P], F32, name="inverse_t")
        for t in range(TILES):
            cols = slice(t * P, (t + 1) * P)
            nc.scalar.activation(root_t[:, cols], total_t[:, cols], ACT.Abs_reciprocal_sqrt)
        inverse = []
        for t in range(TILES):
            cols = slice(t * P, (t + 1) * P)
            nc.scalar.activation(inverse_t[:, cols], root_t[:, cols], ACT.Square)
            back = psum.tile([P, V], F32, name=f"inverse{t}")
            nc.tensor.transpose(back[:], inverse_t[:, cols], identity[:])
            inverse.append(back)
        for t in range(TILES):
            nc.vector.tensor_tensor(mf[t][:], flow_table[t][:].indirect(nbr_sb[:]), ex[t][:], ALU.mult)
        result = pool.tile([P, TILES * V], F32, name="result")
        for t in range(TILES):
            nc.vector.tensor_reduce(num[:, t * V : (t + 1) * V], mf[t][:].rearrange("p (v d) -> p v d", d=D), AX.X, ALU.add)
        for t in range(TILES):
            cols = slice(t * V, (t + 1) * V)
            nc.vector.scalar_tensor_tensor(result[:, cols], num[:, cols], 8.0, inverse[t][:], ALU.mult, ALU.mult)
            nc.sync.dma_start(out[t * P : (t + 1) * P, :], result[:, cols])
